import numpy as np
import ml_dtypes


def mxq(x, axis, fmt="e4m3"):
    dtype, down = {"e4m3": (ml_dtypes.float8_e4m3fn, 7), "e5m2": (ml_dtypes.float8_e5m2, 14)}[fmt]
    v = np.moveaxis(np.asarray(x, np.float32).astype(ml_dtypes.bfloat16).astype(np.float64), axis, -1)
    blocks = v.reshape(v.shape[:-1] + (-1, 32))
    amax = np.abs(blocks).max(-1, keepdims=True)
    byte = np.maximum(np.where(amax > 0, np.frexp(amax)[1] - 1 + 127, 0) - down, 1)
    scale = np.exp2(byte - 127.0)
    codes = (blocks / scale).astype(np.float32).astype(dtype).astype(np.float64)
    return np.moveaxis((codes * scale).reshape(v.shape), -1, axis)


WIDE = False


def mx_kscale(k):
    if not WIDE:
        return np.ones(k)
    levels = np.array([10, -10, 5, -5, 0])
    if k % 512:
        return np.exp2(np.random.permutation(np.resize(levels, k // 32))).repeat(32)
    a = np.empty((k // 512, 16))
    for p in range(k // 512):
        a[p, :8] = np.random.permutation(np.resize(levels, 8))
        for g in range(8):
            far = levels[np.abs(levels - a[p, g]) >= 10]
            a[p, g + 8] = far[np.random.randint(len(far))]
    return np.exp2(a.ravel()).repeat(32)


def f64(x):
    return np.asarray(x).astype(np.float64)


def striped(idx):
    return np.tile(idx.reshape(-1, 16).T, (8, 1)).astype(np.uint16)


def unstriped(offs):
    return offs[:16].T.reshape(-1).astype(np.int64)


E2M1 = np.array([0.0, 0.5, 1.0, 1.5, 2.0, 3.0, 4.0, 6.0, -0.0, -0.5, -1.0, -1.5, -2.0, -3.0, -4.0, -6.0])


def pack_weight(w, fmt):
    k, n = w.shape
    w = f64(np.asarray(w, np.float32).astype(ml_dtypes.bfloat16)).reshape(k // 32, 32, n)
    amax = np.abs(w).max(1)
    if fmt == "e4m3":
        byte = np.frexp(amax)[1] - 1 + 127 - 7
    else:
        mant, ex = np.frexp(amax / 6.0)
        byte = np.where(mant > 0.5, ex, ex - 1) + 127
    byte = np.clip(np.where(amax > 0, byte, 1), 1, 254)
    scaled = (w * np.exp2(127.0 - byte)[:, None, :]).reshape(k, n).astype(np.float32)
    by_word = np.ascontiguousarray(scaled.reshape(k // 512, 128, 4, n).transpose(0, 1, 3, 2))
    if fmt == "e4m3":
        words = by_word.astype(ml_dtypes.float8_e4m3fn).view(np.uint8)
    else:
        c = by_word.astype(ml_dtypes.float4_e2m1fn).view(np.uint8) & 0xF
        words = (c[..., 0::2] | (c[..., 1::2] << 4)).reshape(k // 512, 128, 2 * n)
    return np.ascontiguousarray(words), np.ascontiguousarray(byte.astype(np.uint8).reshape(k // 512, 16, n))


def unpack_weight(words, scales, fmt):
    g, _, n = scales.shape
    words = np.ascontiguousarray(words).reshape(g, 128, n, -1)
    if fmt == "e4m3":
        vals = words.view(ml_dtypes.float8_e4m3fn).astype(np.float64)
    else:
        nib = np.empty((g, 128, n, 4), np.uint8)
        nib[..., 0::2] = words & 0xF
        nib[..., 1::2] = words >> 4
        vals = E2M1[nib]
    vals = vals * np.repeat(np.exp2(scales.astype(np.float64) - 127.0), 8, axis=1)[..., None]
    return vals.transpose(0, 1, 3, 2).reshape(g * 512, n)


def gelu(v):
    return 0.5 * v * (1.0 + np.tanh(np.sqrt(2.0 / np.pi) * (v + 0.044715 * v**3)))


K, T, S, H, N, K2, T2, P = 1024, 4096, 1024, 512, 512, 512, 2048, 512

def setup_inputs():
    n = np.random.standard_normal
    s = mx_kscale(K)[:, None]
    s2 = mx_kscale(K2)[:, None]
    u = mx_kscale(H)[:, None]
    tab_words, tab_scales = pack_weight(n((K, T)) * s, "e4m3")
    tab2_words, tab2_scales = pack_weight(n((K2, T2)) * s2, "e4m3")
    w2_words, w2_scales = pack_weight(n((H, N)) / np.sqrt(H) / u, "e2m1")
    f2_words, f2_scales = pack_weight(n((K2, N)) / np.sqrt(K2) / s2, "e4m3")
    return {
        "tab_words": tab_words, "tab_scales": tab_scales,
        "tab2_words": tab2_words, "tab2_scales": tab2_scales,
        "offs": striped(np.random.permutation(T)[:S]),
        "offs2": striped(np.random.permutation(T2)[:P]),
        "pos1": striped(np.random.permutation(S)[:P]),
        "w1": (0.52 * n((H, K)).T / np.sqrt(K) / s).astype(np.float32),
        "mark": (n((H, S)) * u).astype(np.float32),
        "d": (0.6 * n(H) * u[:, 0]).astype(np.float32),
        "w2_words": w2_words, "w2_scales": w2_scales,
        "w3": (0.6 * n((K, N)) / np.sqrt(K) / s).astype(np.float32),
        "f1": (n((K2, N)) / np.sqrt(K2) / s2).astype(np.float32),
        "f2_words": f2_words, "f2_scales": f2_scales,
    }

def reference(tab_words, tab_scales, tab2_words, tab2_scales, offs, offs2, pos1, w1, mark, d, w2_words, w2_scales, w3, f1, f2_words, f2_scales):
    v = unpack_weight(tab_words, tab_scales, "e4m3")[:, unstriped(offs)]
    v2 = unpack_weight(tab2_words, tab2_scales, "e4m3")[:, unstriped(offs2)]
    w2 = unpack_weight(w2_words, w2_scales, "e2m1")
    f2 = unpack_weight(f2_words, f2_scales, "e4m3")
    h = np.cos(mxq(f64(w1), 0, "e4m3").T @ v) * f64(mark) + f64(d)[:, None]
    hq = mxq(h, 0, "e4m3")
    y = w2.T @ hq + mxq(f64(w3), 0, "e4m3").T @ v
    b1 = mxq(f64(f1), 0, "e4m3").T @ v2
    b2 = f2.T @ v2
    b = np.maximum(b1, b2)
    return y[:, unstriped(pos1)] * b

@@ -1,0 +1,249 @@
+import math
+from contextlib import ExitStack
+
+import concourse.mybir as mybir
+
+K, T, S, H, N, K2, T2, PAIRS = 1024, 4096, 1024, 512, 512, 512, 2048, 512
+FLOPS = 2 * (K * H * S + H * N * S + K * N * S + 2 * K2 * N * PAIRS)
+
+F32 = mybir.dt.float32
+BF16 = mybir.dt.bfloat16
+I32 = mybir.dt.int32
+U32 = mybir.dt.uint32
+U16 = mybir.dt.uint16
+U8 = mybir.dt.uint8
+FP8X4 = mybir.dt.float8_e4m3fn_x4
+FP4X4 = mybir.dt.float4_e2m1fn_x4
+ALU = mybir.AluOpType
+ACT = mybir.ActivationFunctionType
+
+P = 128
+PACK = 4
+K_PASS = P * PACK
+COLS = 512
+HALVES = S // COLS
+UNIT = 128
+ROUND = 1.5 * 2.0**23
+
+
+def tile_list_lesion_history_features_kernel(
+    tc, tab_words, tab_scales, tab2_words, tab2_scales, offs, offs2, pos1,
+    w1, mark, d, w2_words, w2_scales, w3, f1, f2_words, f2_scales, out,
+):
+    nc = tc.nc
+    passes = K // K_PASS
+
+    with ExitStack() as ctx:
+        keep = ctx.enter_context(tc.tile_pool(name="keep", bufs=1))
+        ring = ctx.enter_context(tc.tile_pool(name="ring", bufs=3))
+        psum = ctx.enter_context(tc.psum_pool(name="psum", bufs=1))
+
+        def held(name, shape, dtype):
+            return keep.tile(shape, dtype, name=name, align_bytes=64)
+
+        def load_words(name, words):
+            tile = held(name, [P, words.shape[1]], I32)
+            nc.sync.dma_start(out=tile[:], in_=words.rearrange("p t i -> p (t i)").bitcast(I32))
+            return tile
+
+        def load_scales(name, scales, clear, queue):
+            count, width = scales.shape[0], scales.shape[2]
+            tile = held(name, [P, width], U8)
+            clear.memset(tile[:].bitcast(I32), 0)
+            for q in range(4):
+                queue.dma_start(
+                    out=tile[32 * q : 32 * q + 4 * count, :].bitcast(I32),
+                    in_=scales[:, 4 * q : 4 * q + 4, :].bitcast(I32),
+                )
+            return tile
+
+        def load_rows(name, rows):
+            tile = held(name, [P, PACK, rows.shape[1]], F32)
+            nc.sync.dma_start(out=tile[:], in_=rows.rearrange("(p j) c -> p j c", j=PACK))
+            return tile
+
+        def load_list(name, values):
+            tile = keep.tile([P, values.shape[1]], U16, name=name)
+            nc.sync.dma_start(tile[:], values)
+            return tile
+
+        def quantise(name, grouped):
+            codes = held(name + "_codes", [P, COLS], U32)
+            scales = held(name + "_scales", [P, COLS], U8)
+            nc.vector.quantize_mx(out=codes[:].bitcast(FP8X4), scales=scales[:], in_=grouped[:])
+            return codes, scales
+
+        def group_plain(name, raw, copy):
+            grouped = held(name + "_grouped", [P, PACK * COLS], BF16)
+            copy(
+                out=grouped[:].rearrange("p (c i j) -> p c j i", i=2, j=PACK),
+                in_=raw[:].rearrange("p j (c i) -> p c j i", i=2),
+            )
+            return grouped
+
+        def group_dealt(name, raw):
+            grouped = held(name + "_grouped", [P, PACK * COLS], BF16)
+            nc.scalar.copy(
+                out=grouped[:].rearrange("p (t m j) -> p m t j", t=PACK, j=PACK),
+                in_=raw[:].rearrange("p j (m t) -> p m t j", t=PACK),
+            )
+            return grouped
+
+        def gather(name, window, offsets, dtype):
+            picked = held(name, [P, COLS], dtype)
+            nc.vector.tensor_copy(picked[:], window.indirect(offsets))
+            return picked
+
+        def product(acc, lhs, lhs_scale, rhs, rhs_scale, start, stop):
+            nc.tensor.matmul_mx(out=acc, lhsT=lhs, lhsT_scale=lhs_scale, rhs=rhs, rhs_scale=rhs_scale,
+                                start=start, stop=stop)
+
+        idx = load_list("idx", offs)
+        tab_planes = load_scales("tab_planes", tab_scales, nc.vector, nc.scalar)
+        tab = [load_words("tab0", tab_words[0])]
+        w1_raw = [load_rows("w1_raw%d" % a, w1[a * K_PASS : (a + 1) * K_PASS, :]) for a in range(passes)]
+        tab.append(load_words("tab1", tab_words[1]))
+        marks = [load_rows("mark0", mark[:, 0:COLS])]
+        shift = held("shift", [P, PACK], F32)
+        nc.sync.dma_start(out=shift[:], in_=d.rearrange("(p t) -> p t", t=PACK))
+        idx2 = load_list("idx2", offs2)
+        tab2 = load_words("tab2", tab2_words[0])
+        tab2_planes = load_scales("tab2_planes", tab2_scales, nc.gpsimd, nc.sync)
+        f1_raw = load_rows("f1_raw", f1)
+        f2_planes = load_scales("f2_planes", f2_scales, nc.gpsimd, nc.sync)
+        f2_codes = load_words("f2_codes", f2_words[0])
+        marks.append(load_rows("mark1", mark[:, COLS:S]))
+        w3_raw = [load_rows("w3_raw%d" % a, w3[a * K_PASS : (a + 1) * K_PASS, :]) for a in range(passes)]
+        w2_planes = load_scales("w2_planes", w2_scales, nc.gpsimd, nc.sync)
+        w2_codes = held("w2_codes", [P, 2 * N], U8)
+        nc.sync.dma_start(out=w2_codes[:].bitcast(I32), in_=w2_words[0].bitcast(I32))
+        p1 = load_list("p1", pos1)
+
+        def part(h):
+            return idx[:, h * (COLS // 16) : (h + 1) * (COLS // 16)]
+
+        v_codes = {}
+        for h in range(HALVES):
+            v_codes[0, h] = gather("v_codes0%d" % h, tab[0][:].bitcast(U32), part(h), U32)
+        w1_q = [quantise("w1q0", group_dealt("w10", w1_raw[0]))]
+        v_scales = [gather("v_scales%d" % h, tab_planes[:], part(h), U8) for h in range(HALVES)]
+        w1_q.append(quantise("w1q1", group_dealt("w11", w1_raw[1])))
+        for h in range(HALVES):
+            v_codes[1, h] = gather("v_codes1%d" % h, tab[1][:].bitcast(U32), part(h), U32)
+
+        def v_pass(acc, weight, cols, a, h, picked, start, stop):
+            codes, scales = weight[a]
+            product(acc, codes[:, cols].bitcast(FP8X4), scales[:, cols],
+                    v_codes[a, h][:, picked].bitcast(FP8X4), v_scales[h][4 * a :, picked], start, stop)
+
+        per_half = COLS // UNIT
+        units = S // UNIT
+        turns, whole, cosine, grouped_h = {}, {}, {}, {}
+        h_codes = [held("h_codes%d" % h, [P, COLS], U32) for h in range(HALVES)]
+        h_scales = [held("h_scales%d" % h, [P, COLS], U8) for h in range(HALVES)]
+
+        def place(u):
+            return u // per_half, slice(UNIT * (u % per_half), UNIT * (u % per_half + 1))
+
+        def angle(u):
+            h, picked = place(u)
+            z = psum.tile([P, PACK, UNIT], F32, name="z", bufs=2)
+            for t in range(PACK):
+                for a in range(passes):
+                    v_pass(z[:, t, :], w1_q, slice(P * t, P * (t + 1)), a, h, picked, a == 0, a == passes - 1)
+            turns[u] = held("turns%d" % u, [P, PACK, UNIT], F32)
+            nc.scalar.activation(turns[u][:], z[:], ACT.Copy, bias=0.25, scale=1.0 / (2.0 * math.pi))
+            whole[u] = held("whole%d" % u, [P, PACK, UNIT], F32)
+            nc.scalar.activation(whole[u][:], turns[u][:], ACT.Copy, bias=ROUND, scale=1.0)
+
+        def cos_of(u):
+            nc.vector.scalar_tensor_tensor(whole[u][:], whole[u][:], ROUND, turns[u][:], ALU.subtract, ALU.subtract)
+            cosine[u] = held("cosine%d" % u, [P, PACK, UNIT], F32)
+            nc.scalar.activation(cosine[u][:], whole[u][:], ACT.Sin, scale=-2.0 * math.pi)
+
+        def marked(u):
+            h, picked = place(u)
+            nc.vector.tensor_tensor(cosine[u][:], cosine[u][:], marks[h][:, :, picked], ALU.mult)
+
+        def group_h(u):
+            grouped_h[u] = ring.tile([P, PACK * UNIT], BF16, name="grouped_h", align_bytes=64)
+            nc.vector.tensor_tensor(
+                grouped_h[u][:].rearrange("p (c i t) -> p c t i", i=2, t=PACK),
+                cosine[u][:].rearrange("p t (c i) -> p c t i", i=2),
+                shift[:].unsqueeze(1).unsqueeze(3).to_broadcast([P, UNIT // 2, PACK, 2]),
+                ALU.add,
+            )
+
+        def quantise_h(u):
+            h, picked = place(u)
+            nc.vector.quantize_mx(out=h_codes[h][:, picked].bitcast(FP8X4), scales=h_scales[h][:, picked],
+                                  in_=grouped_h[u][:])
+
+        y = [held("y%d" % n, [P, S], F32) for n in range(N // P)]
+        sums = {}
+
+        def second_open(h):
+            for n in range(N // P):
+                sums[h, n] = psum.tile([P, COLS], F32, name="acc", bufs=4)
+                for a in range(passes):
+                    v_pass(sums[h, n][:], w3_q, slice(P * n, P * (n + 1)), a, h, slice(0, COLS), a == 0, False)
+
+        def second_close(h):
+            for n in range(N // P):
+                product(sums[h, n][:], w2_codes[:, 2 * P * n : 2 * P * (n + 1)].bitcast(FP4X4),
+                        w2_planes[:, P * n : P * (n + 1)], h_codes[h][:].bitcast(FP8X4), h_scales[h][:], False, True)
+                nc.scalar.copy(out=y[n][:, h * COLS : (h + 1) * COLS], in_=sums[h, n][:])
+
+        second, larger = {}, {}
+
+        def readings(n):
+            cols = slice(P * n, P * (n + 1))
+            first = psum.tile([P, COLS], F32, name="first")
+            product(first[:], f1_q[0][:, cols].bitcast(FP8X4), f1_q[1][:, cols],
+                    v2_codes[:].bitcast(FP8X4), v2_scales[:], True, True)
+            second[n] = psum.tile([P, COLS], F32, name="second")
+            product(second[n][:], f2_codes[:, cols].bitcast(FP8X4), f2_planes[:, cols],
+                    v2_codes[:].bitcast(FP8X4), v2_scales[:], True, True)
+            larger[n] = held("larger%d" % n, [P, COLS], F32)
+            nc.scalar.copy(out=larger[n][:], in_=first[:])
+
+        def take_larger(n):
+            nc.vector.tensor_tensor(larger[n][:], second[n][:], larger[n][:], ALU.max)
+
+        w3_grouped, w3_q = [], []
+        for i in range(units + 4):
+            if i < units:
+                angle(i)
+            if 1 <= i < units + 1:
+                cos_of(i - 1)
+            if i >= 4:
+                quantise_h(i - 4)
+            if 2 <= i < units + 2:
+                marked(i - 2)
+            if 3 <= i < units + 3:
+                group_h(i - 3)
+            if i == 1:
+                v2_codes = gather("v2_codes", tab2[:].bitcast(U32), idx2[:], U32)
+            if i == 2:
+                v2_scales = gather("v2_scales", tab2_planes[:], idx2[:], U8)
+                f1_grouped = group_plain("f1", f1_raw, nc.vector.tensor_copy)
+            if i == 3:
+                f1_q = quantise("f1q", f1_grouped)
+            if 5 <= i < 9:
+                take_larger(i - 5)
+            if 4 <= i < 8:
+                readings(i - 4)
+            if i in (4, 5):
+                w3_grouped.append(group_plain("w3%d" % (i - 4), w3_raw[i - 4], nc.scalar.copy))
+            if i in (6, 7):
+                w3_q.append(quantise("w3q%d" % (i - 6), w3_grouped[i - 6]))
+            if i == 7:
+                second_open(0)
+                second_close(0)
+            if i == 9:
+                second_open(1)
+        second_close(1)
+        for n in range(N // P):
+            result = ring.tile([P, PAIRS], F32, name="result")
+            nc.vector.tensor_tensor(result[:], y[n][:].indirect(p1[:]), larger[n][:], ALU.mult)
+            nc.sync.dma_start(out=out[P * n : P * (n + 1), :], in_=result[:])

@@ -23,7 +23,6 @@ K_PASS = P * PACK
 COLS = 512
 HALVES = S // COLS
 UNIT = 128
-ROUND = 1.5 * 2.0**23
 
 
 def tile_list_lesion_history_features_kernel(
@@ -38,23 +37,29 @@ def tile_list_lesion_history_features_kernel(
         ring = ctx.enter_context(tc.tile_pool(name="ring", bufs=3))
         psum = ctx.enter_context(tc.psum_pool(name="psum", bufs=1))
 
-        def held(name, shape, dtype):
-            return keep.tile(shape, dtype, name=name, align_bytes=64)
+        def held(name, shape, dtype, tag=None):
+            return keep.tile(shape, dtype, name=name, tag=tag or name, align_bytes=64)
 
         def load_words(name, words):
             tile = held(name, [P, words.shape[1]], I32)
             nc.sync.dma_start(out=tile[:], in_=words.rearrange("p t i -> p (t i)").bitcast(I32))
             return tile
 
-        def load_scales(name, scales, clear, queue):
-            count, width = scales.shape[0], scales.shape[2]
+        def cleared(name, width, engine):
             tile = held(name, [P, width], U8)
-            clear.memset(tile[:].bitcast(I32), 0)
+            engine.memset(tile[:].bitcast(I32), 0)
+            return tile
+
+        def load_plane(tile, scales, a):
             for q in range(4):
-                queue.dma_start(
-                    out=tile[32 * q : 32 * q + 4 * count, :].bitcast(I32),
-                    in_=scales[:, 4 * q : 4 * q + 4, :].bitcast(I32),
+                nc.sync.dma_start(
+                    out=tile[32 * q + 4 * a : 32 * q + 4 * a + 4, :].bitcast(I32),
+                    in_=scales[a, 4 * q : 4 * q + 4, :].bitcast(I32),
                 )
+
+        def load_scales(name, scales):
+            tile = cleared(name, scales.shape[2], nc.gpsimd)
+            load_plane(tile, scales, 0)
             return tile
 
         def load_rows(name, rows):
@@ -76,8 +81,8 @@ def tile_list_lesion_history_features_kernel(
         def group_plain(name, raw, copy):
             grouped = held(name + "_grouped", [P, PACK * COLS], BF16)
             copy(
-                out=grouped[:].rearrange("p (c i j) -> p c j i", i=2, j=PACK),
-                in_=raw[:].rearrange("p j (c i) -> p c j i", i=2),
+                out=grouped[:].rearrange("p (c i j) -> p c j i", i=4, j=PACK),
+                in_=raw[:].rearrange("p j (c i) -> p c j i", i=4),
             )
             return grouped
 
@@ -98,38 +103,32 @@ def tile_list_lesion_history_features_kernel(
             nc.tensor.matmul_mx(out=acc, lhsT=lhs, lhsT_scale=lhs_scale, rhs=rhs, rhs_scale=rhs_scale,
                                 start=start, stop=stop)
 
+        idx2 = load_list("idx2", offs2)
+        tab2 = load_words("tab2", tab2_words[0])
+        tab2_planes = load_scales("tab2_planes", tab2_scales)
+        f1_raw = load_rows("f1_raw", f1)
+        f2_planes = load_scales("f2_planes", f2_scales)
+        f2_codes = load_words("f2_codes", f2_words[0])
         idx = load_list("idx", offs)
-        tab_planes = load_scales("tab_planes", tab_scales, nc.vector, nc.scalar)
         tab = [load_words("tab0", tab_words[0])]
-        w1_raw = [load_rows("w1_raw%d" % a, w1[a * K_PASS : (a + 1) * K_PASS, :]) for a in range(passes)]
+        tab_planes = cleared("tab_planes", T, nc.vector)
+        w1_raw = []
+        for a in range(passes):
+            load_plane(tab_planes, tab_scales, a)
+            w1_raw.append(load_rows("w1_raw%d" % a, w1[a * K_PASS : (a + 1) * K_PASS, :]))
         tab.append(load_words("tab1", tab_words[1]))
         marks = [load_rows("mark0", mark[:, 0:COLS])]
         shift = held("shift", [P, PACK], F32)
         nc.sync.dma_start(out=shift[:], in_=d.rearrange("(p t) -> p t", t=PACK))
-        idx2 = load_list("idx2", offs2)
-        tab2 = load_words("tab2", tab2_words[0])
-        tab2_planes = load_scales("tab2_planes", tab2_scales, nc.gpsimd, nc.sync)
-        f1_raw = load_rows("f1_raw", f1)
-        f2_planes = load_scales("f2_planes", f2_scales, nc.gpsimd, nc.sync)
-        f2_codes = load_words("f2_codes", f2_words[0])
-        marks.append(load_rows("mark1", mark[:, COLS:S]))
         w3_raw = [load_rows("w3_raw%d" % a, w3[a * K_PASS : (a + 1) * K_PASS, :]) for a in range(passes)]
-        w2_planes = load_scales("w2_planes", w2_scales, nc.gpsimd, nc.sync)
+        marks.append(load_rows("mark1", mark[:, COLS:S]))
+        w2_planes = load_scales("w2_planes", w2_scales)
         w2_codes = held("w2_codes", [P, 2 * N], U8)
         nc.sync.dma_start(out=w2_codes[:].bitcast(I32), in_=w2_words[0].bitcast(I32))
         p1 = load_list("p1", pos1)
 
         def part(h):
             return idx[:, h * (COLS // 16) : (h + 1) * (COLS // 16)]
-
-        v_codes = {}
-        for h in range(HALVES):
-            v_codes[0, h] = gather("v_codes0%d" % h, tab[0][:].bitcast(U32), part(h), U32)
-        w1_q = [quantise("w1q0", group_dealt("w10", w1_raw[0]))]
-        v_scales = [gather("v_scales%d" % h, tab_planes[:], part(h), U8) for h in range(HALVES)]
-        w1_q.append(quantise("w1q1", group_dealt("w11", w1_raw[1])))
-        for h in range(HALVES):
-            v_codes[1, h] = gather("v_codes1%d" % h, tab[1][:].bitcast(U32), part(h), U32)
 
         def v_pass(acc, weight, cols, a, h, picked, start, stop):
             codes, scales = weight[a]
@@ -138,7 +137,7 @@ def tile_list_lesion_history_features_kernel(
 
         per_half = COLS // UNIT
         units = S // UNIT
-        turns, whole, cosine, grouped_h = {}, {}, {}, {}
+        angles, whole, cosine, rounded, grouped_h = {}, {}, {}, {}, {}
         h_codes = [held("h_codes%d" % h, [P, COLS], U32) for h in range(HALVES)]
         h_scales = [held("h_scales%d" % h, [P, COLS], U8) for h in range(HALVES)]
 
@@ -147,31 +146,42 @@ def tile_list_lesion_history_features_kernel(
 
         def angle(u):
             h, picked = place(u)
-            z = psum.tile([P, PACK, UNIT], F32, name="z", bufs=2)
-            for t in range(PACK):
-                for a in range(passes):
-                    v_pass(z[:, t, :], w1_q, slice(P * t, P * (t + 1)), a, h, picked, a == 0, a == passes - 1)
-            turns[u] = held("turns%d" % u, [P, PACK, UNIT], F32)
-            nc.scalar.activation(turns[u][:], z[:], ACT.Copy, bias=0.25, scale=1.0 / (2.0 * math.pi))
-            whole[u] = held("whole%d" % u, [P, PACK, UNIT], F32)
-            nc.scalar.activation(whole[u][:], turns[u][:], ACT.Copy, bias=ROUND, scale=1.0)
+            z = psum.tile([P, PACK, UNIT], F32, name="z", tag="bank%d" % (u % 4))
+            for a in range(passes):
+                for t in range(PACK):
+                    v_pass(z[:, t, :], w1_q, slice(P * t, P * (t + 1)), a, h, picked,
+                           (a, t) == (0, 0), (a, t) == (passes - 1, PACK - 1))
+            angles[u] = z
+            whole[u] = held("whole%d" % u, [P, PACK, UNIT], I32)
+            nc.vector.tensor_scalar(whole[u][:], z[:], 1.0 / (2.0 * math.pi), 0.25, ALU.mult, ALU.add)
 
         def cos_of(u):
-            nc.vector.scalar_tensor_tensor(whole[u][:], whole[u][:], ROUND, turns[u][:], ALU.subtract, ALU.subtract)
-            cosine[u] = held("cosine%d" % u, [P, PACK, UNIT], F32)
-            nc.scalar.activation(cosine[u][:], whole[u][:], ACT.Sin, scale=-2.0 * math.pi)
+            rest = held("rest%d" % u, [P, PACK, UNIT], F32)
+            nc.vector.scalar_tensor_tensor(rest[:], angles[u][:], 1.0 / (2.0 * math.pi), whole[u][:],
+                                           ALU.mult, ALU.subtract)
+            cosine[u] = held("cosine%d" % u, [P, PACK, UNIT], F32, "whole%d" % u)
+            nc.scalar.activation(cosine[u][:], rest[:], ACT.Sin, bias=math.pi / 2.0, scale=2.0 * math.pi)
 
         def marked(u):
             h, picked = place(u)
-            nc.vector.tensor_tensor(cosine[u][:], cosine[u][:], marks[h][:, :, picked], ALU.mult)
+            engine = nc.gpsimd if u < units - 1 else nc.vector
+            engine.tensor_tensor(cosine[u][:], cosine[u][:], marks[h][:, :, picked], ALU.mult)
+
+        def shifted(u):
+            rounded[u] = ring.tile([P, PACK, UNIT], BF16, name="rounded")
+            for t in range(PACK):
+                if u < units - 1:
+                    nc.scalar.activation(rounded[u][:, t, :], cosine[u][:, t, :], ACT.Identity,
+                                         bias=shift[:, t : t + 1])
+                else:
+                    nc.vector.tensor_scalar(rounded[u][:, t, :], cosine[u][:, t, :], shift[:, t : t + 1], None,
+                                            ALU.add)
 
         def group_h(u):
             grouped_h[u] = ring.tile([P, PACK * UNIT], BF16, name="grouped_h", align_bytes=64)
-            nc.vector.tensor_tensor(
-                grouped_h[u][:].rearrange("p (c i t) -> p c t i", i=2, t=PACK),
-                cosine[u][:].rearrange("p t (c i) -> p c t i", i=2),
-                shift[:].unsqueeze(1).unsqueeze(3).to_broadcast([P, UNIT // 2, PACK, 2]),
-                ALU.add,
+            nc.vector.tensor_copy(
+                grouped_h[u][:].rearrange("p (c i t) -> p c t i", i=4, t=PACK),
+                rounded[u][:].rearrange("p t (c i) -> p c t i", i=4),
             )
 
         def quantise_h(u):
@@ -184,7 +194,7 @@ def tile_list_lesion_history_features_kernel(
 
         def second_open(h):
             for n in range(N // P):
-                sums[h, n] = psum.tile([P, COLS], F32, name="acc", bufs=4)
+                sums[h, n] = psum.tile([P, COLS], F32, name="acc", tag="bank%d" % (n + 4 * (1 - h)))
                 for a in range(passes):
                     v_pass(sums[h, n][:], w3_q, slice(P * n, P * (n + 1)), a, h, slice(0, COLS), a == 0, False)
 
@@ -198,10 +208,10 @@ def tile_list_lesion_history_features_kernel(
 
         def readings(n):
             cols = slice(P * n, P * (n + 1))
-            first = psum.tile([P, COLS], F32, name="first")
+            first = psum.tile([P, COLS], F32, name="first", tag="bank%d" % (2 * n))
             product(first[:], f1_q[0][:, cols].bitcast(FP8X4), f1_q[1][:, cols],
                     v2_codes[:].bitcast(FP8X4), v2_scales[:], True, True)
-            second[n] = psum.tile([P, COLS], F32, name="second")
+            second[n] = psum.tile([P, COLS], F32, name="second", tag="bank%d" % (2 * n + 1))
             product(second[n][:], f2_codes[:, cols].bitcast(FP8X4), f2_planes[:, cols],
                     v2_codes[:].bitcast(FP8X4), v2_scales[:], True, True)
             larger[n] = held("larger%d" % n, [P, COLS], F32)
@@ -210,34 +220,41 @@ def tile_list_lesion_history_features_kernel(
         def take_larger(n):
             nc.vector.tensor_tensor(larger[n][:], second[n][:], larger[n][:], ALU.max)
 
+        v2_codes = gather("v2_codes", tab2[:].bitcast(U32), idx2[:], U32)
+        f1_q = quantise("f1q", group_plain("f1", f1_raw, nc.scalar.copy))
+        v2_scales = gather("v2_scales", tab2_planes[:], idx2[:], U8)
+        for n in range(N // P):
+            readings(n)
+            take_larger(n)
+
+        v_codes = {}
+        for h in range(HALVES):
+            v_codes[0, h] = gather("v_codes0%d" % h, tab[0][:].bitcast(U32), part(h), U32)
+        w1_q = [quantise("w1q0", group_dealt("w10", w1_raw[0]))]
+        v_scales = [gather("v_scales%d" % h, tab_planes[:], part(h), U8) for h in range(HALVES)]
+        w1_q.append(quantise("w1q1", group_dealt("w11", w1_raw[1])))
+        for h in range(HALVES):
+            v_codes[1, h] = gather("v_codes1%d" % h, tab[1][:].bitcast(U32), part(h), U32)
+
         w3_grouped, w3_q = [], []
-        for i in range(units + 4):
+        for i in range(units + 5):
             if i < units:
                 angle(i)
             if 1 <= i < units + 1:
                 cos_of(i - 1)
-            if i >= 4:
-                quantise_h(i - 4)
             if 2 <= i < units + 2:
                 marked(i - 2)
             if 3 <= i < units + 3:
-                group_h(i - 3)
-            if i == 1:
-                v2_codes = gather("v2_codes", tab2[:].bitcast(U32), idx2[:], U32)
-            if i == 2:
-                v2_scales = gather("v2_scales", tab2_planes[:], idx2[:], U8)
-                f1_grouped = group_plain("f1", f1_raw, nc.vector.tensor_copy)
-            if i == 3:
-                f1_q = quantise("f1q", f1_grouped)
-            if 5 <= i < 9:
-                take_larger(i - 5)
-            if 4 <= i < 8:
-                readings(i - 4)
-            if i in (4, 5):
-                w3_grouped.append(group_plain("w3%d" % (i - 4), w3_raw[i - 4], nc.scalar.copy))
-            if i in (6, 7):
-                w3_q.append(quantise("w3q%d" % (i - 6), w3_grouped[i - 6]))
-            if i == 7:
+                shifted(i - 3)
+            if 4 <= i < units + 4:
+                group_h(i - 4)
+            if i >= 5:
+                quantise_h(i - 5)
+            if i in (2, 4):
+                w3_grouped.append(group_plain("w3%d" % (i // 2 - 1), w3_raw[i // 2 - 1], nc.scalar.copy))
+            if i in (4, 6):
+                w3_q.append(quantise("w3q%d" % (i // 2 - 2), w3_grouped[i // 2 - 2]))
+            if i == 8:
                 second_open(0)
                 second_close(0)
             if i == 9:

import math
from contextlib import ExitStack

import concourse.mybir as mybir

K, T, S, H, N, K2, T2, PAIRS = 1024, 4096, 1024, 512, 512, 512, 2048, 512
FLOPS = 2 * (K * H * S + H * N * S + K * N * S + 2 * K2 * N * PAIRS)

F32 = mybir.dt.float32
BF16 = mybir.dt.bfloat16
I32 = mybir.dt.int32
U32 = mybir.dt.uint32
U16 = mybir.dt.uint16
U8 = mybir.dt.uint8
FP8X4 = mybir.dt.float8_e4m3fn_x4
FP4X4 = mybir.dt.float4_e2m1fn_x4
ALU = mybir.AluOpType
ACT = mybir.ActivationFunctionType

P = 128
PACK = 4
K_PASS = P * PACK
COLS = 512
HALVES = S // COLS
UNIT = 128


def tile_list_lesion_history_features_kernel(
    tc, tab_words, tab_scales, tab2_words, tab2_scales, offs, offs2, pos1,
    w1, mark, d, w2_words, w2_scales, w3, f1, f2_words, f2_scales, out,
):
    nc = tc.nc
    passes = K // K_PASS

    with ExitStack() as ctx:
        keep = ctx.enter_context(tc.tile_pool(name="keep", bufs=1))
        ring = ctx.enter_context(tc.tile_pool(name="ring", bufs=3))
        psum = ctx.enter_context(tc.psum_pool(name="psum", bufs=1))

        def held(name, shape, dtype, tag=None):
            return keep.tile(shape, dtype, name=name, tag=tag or name, align_bytes=64)

        def load_words(name, words):
            tile = held(name, [P, words.shape[1]], I32)
            nc.sync.dma_start(out=tile[:], in_=words.rearrange("p t i -> p (t i)").bitcast(I32))
            return tile

        def cleared(name, width, engine):
            tile = held(name, [P, width], U8)
            engine.memset(tile[:].bitcast(I32), 0)
            return tile

        def load_plane(tile, scales, a):
            for q in range(4):
                nc.sync.dma_start(
                    out=tile[32 * q + 4 * a : 32 * q + 4 * a + 4, :].bitcast(I32),
                    in_=scales[a, 4 * q : 4 * q + 4, :].bitcast(I32),
                )

        def load_scales(name, scales):
            tile = cleared(name, scales.shape[2], nc.gpsimd)
            load_plane(tile, scales, 0)
            return tile

        def load_rows(name, rows):
            tile = held(name, [P, PACK, rows.shape[1]], F32)
            nc.sync.dma_start(out=tile[:], in_=rows.rearrange("(p j) c -> p j c", j=PACK))
            return tile

        def load_list(name, values):
            tile = keep.tile([P, values.shape[1]], U16, name=name)
            nc.sync.dma_start(tile[:], values)
            return tile

        def quantise(name, grouped):
            codes = held(name + "_codes", [P, COLS], U32)
            scales = held(name + "_scales", [P, COLS], U8)
            nc.vector.quantize_mx(out=codes[:].bitcast(FP8X4), scales=scales[:], in_=grouped[:])
            return codes, scales

        def group_plain(name, raw, copy):
            grouped = held(name + "_grouped", [P, PACK * COLS], BF16)
            copy(
                out=grouped[:].rearrange("p (c i j) -> p c j i", i=4, j=PACK),
                in_=raw[:].rearrange("p j (c i) -> p c j i", i=4),
            )
            return grouped

        def group_dealt(name, raw):
            grouped = held(name + "_grouped", [P, PACK * COLS], BF16)
            nc.scalar.copy(
                out=grouped[:].rearrange("p (t m j) -> p m t j", t=PACK, j=PACK),
                in_=raw[:].rearrange("p j (m t) -> p m t j", t=PACK),
            )
            return grouped

        def gather(name, window, offsets, dtype):
            picked = held(name, [P, COLS], dtype)
            nc.vector.tensor_copy(picked[:], window.indirect(offsets))
            return picked

        def product(acc, lhs, lhs_scale, rhs, rhs_scale, start, stop):
            nc.tensor.matmul_mx(out=acc, lhsT=lhs, lhsT_scale=lhs_scale, rhs=rhs, rhs_scale=rhs_scale,
                                start=start, stop=stop)

        idx2 = load_list("idx2", offs2)
        tab2 = load_words("tab2", tab2_words[0])
        tab2_planes = load_scales("tab2_planes", tab2_scales)
        f1_raw = load_rows("f1_raw", f1)
        f2_planes = load_scales("f2_planes", f2_scales)
        f2_codes = load_words("f2_codes", f2_words[0])
        idx = load_list("idx", offs)
        tab = [load_words("tab0", tab_words[0])]
        tab_planes = cleared("tab_planes", T, nc.vector)
        w1_raw = []
        for a in range(passes):
            load_plane(tab_planes, tab_scales, a)
            w1_raw.append(load_rows("w1_raw%d" % a, w1[a * K_PASS : (a + 1) * K_PASS, :]))
        tab.append(load_words("tab1", tab_words[1]))
        marks = [load_rows("mark0", mark[:, 0:COLS])]
        shift = held("shift", [P, PACK], F32)
        nc.sync.dma_start(out=shift[:], in_=d.rearrange("(p t) -> p t", t=PACK))
        w3_raw = [load_rows("w3_raw%d" % a, w3[a * K_PASS : (a + 1) * K_PASS, :]) for a in range(passes)]
        marks.append(load_rows("mark1", mark[:, COLS:S]))
        w2_planes = load_scales("w2_planes", w2_scales)
        w2_codes = held("w2_codes", [P, 2 * N], U8)
        nc.sync.dma_start(out=w2_codes[:].bitcast(I32), in_=w2_words[0].bitcast(I32))
        p1 = load_list("p1", pos1)

        def part(h):
            return idx[:, h * (COLS // 16) : (h + 1) * (COLS // 16)]

        def v_pass(acc, weight, cols, a, h, picked, start, stop):
            codes, scales = weight[a]
            product(acc, codes[:, cols].bitcast(FP8X4), scales[:, cols],
                    v_codes[a, h][:, picked].bitcast(FP8X4), v_scales[h][4 * a :, picked], start, stop)

        per_half = COLS // UNIT
        units = S // UNIT
        angles, whole, cosine, rounded, grouped_h = {}, {}, {}, {}, {}
        h_codes = [held("h_codes%d" % h, [P, COLS], U32) for h in range(HALVES)]
        h_scales = [held("h_scales%d" % h, [P, COLS], U8) for h in range(HALVES)]

        def place(u):
            return u // per_half, slice(UNIT * (u % per_half), UNIT * (u % per_half + 1))

        def angle(u):
            h, picked = place(u)
            z = psum.tile([P, PACK, UNIT], F32, name="z", tag="bank%d" % (u % 4))
            for a in range(passes):
                for t in range(PACK):
                    v_pass(z[:, t, :], w1_q, slice(P * t, P * (t + 1)), a, h, picked,
                           (a, t) == (0, 0), (a, t) == (passes - 1, PACK - 1))
            angles[u] = z
            whole[u] = held("whole%d" % u, [P, PACK, UNIT], I32)
            nc.vector.tensor_scalar(whole[u][:], z[:], 1.0 / (2.0 * math.pi), 0.25, ALU.mult, ALU.add)

        def cos_of(u):
            rest = held("rest%d" % u, [P, PACK, UNIT], F32)
            nc.vector.scalar_tensor_tensor(rest[:], angles[u][:], 1.0 / (2.0 * math.pi), whole[u][:],
                                           ALU.mult, ALU.subtract)
            cosine[u] = held("cosine%d" % u, [P, PACK, UNIT], F32, "whole%d" % u)
            nc.scalar.activation(cosine[u][:], rest[:], ACT.Sin, bias=math.pi / 2.0, scale=2.0 * math.pi)

        def marked(u):
            h, picked = place(u)
            engine = nc.gpsimd if u < units - 1 else nc.vector
            engine.tensor_tensor(cosine[u][:], cosine[u][:], marks[h][:, :, picked], ALU.mult)

        def shifted(u):
            rounded[u] = ring.tile([P, PACK, UNIT], BF16, name="rounded")
            for t in range(PACK):
                if u < units - 1:
                    nc.scalar.activation(rounded[u][:, t, :], cosine[u][:, t, :], ACT.Identity,
                                         bias=shift[:, t : t + 1])
                else:
                    nc.vector.tensor_scalar(rounded[u][:, t, :], cosine[u][:, t, :], shift[:, t : t + 1], None,
                                            ALU.add)

        def group_h(u):
            grouped_h[u] = ring.tile([P, PACK * UNIT], BF16, name="grouped_h", align_bytes=64)
            nc.vector.tensor_copy(
                grouped_h[u][:].rearrange("p (c i t) -> p c t i", i=4, t=PACK),
                rounded[u][:].rearrange("p t (c i) -> p c t i", i=4),
            )

        def quantise_h(u):
            h, picked = place(u)
            nc.vector.quantize_mx(out=h_codes[h][:, picked].bitcast(FP8X4), scales=h_scales[h][:, picked],
                                  in_=grouped_h[u][:])

        y = [held("y%d" % n, [P, S], F32) for n in range(N // P)]
        sums = {}

        def second_open(h):
            for n in range(N // P):
                sums[h, n] = psum.tile([P, COLS], F32, name="acc", tag="bank%d" % (n + 4 * (1 - h)))
                for a in range(passes):
                    v_pass(sums[h, n][:], w3_q, slice(P * n, P * (n + 1)), a, h, slice(0, COLS), a == 0, False)

        def second_close(h):
            for n in range(N // P):
                product(sums[h, n][:], w2_codes[:, 2 * P * n : 2 * P * (n + 1)].bitcast(FP4X4),
                        w2_planes[:, P * n : P * (n + 1)], h_codes[h][:].bitcast(FP8X4), h_scales[h][:], False, True)
                nc.scalar.copy(out=y[n][:, h * COLS : (h + 1) * COLS], in_=sums[h, n][:])

        second, larger = {}, {}

        def readings(n):
            cols = slice(P * n, P * (n + 1))
            first = psum.tile([P, COLS], F32, name="first", tag="bank%d" % (2 * n))
            product(first[:], f1_q[0][:, cols].bitcast(FP8X4), f1_q[1][:, cols],
                    v2_codes[:].bitcast(FP8X4), v2_scales[:], True, True)
            second[n] = psum.tile([P, COLS], F32, name="second", tag="bank%d" % (2 * n + 1))
            product(second[n][:], f2_codes[:, cols].bitcast(FP8X4), f2_planes[:, cols],
                    v2_codes[:].bitcast(FP8X4), v2_scales[:], True, True)
            larger[n] = held("larger%d" % n, [P, COLS], F32)
            nc.scalar.copy(out=larger[n][:], in_=first[:])

        def take_larger(n):
            nc.vector.tensor_tensor(larger[n][:], second[n][:], larger[n][:], ALU.max)

        v2_codes = gather("v2_codes", tab2[:].bitcast(U32), idx2[:], U32)
        f1_q = quantise("f1q", group_plain("f1", f1_raw, nc.scalar.copy))
        v2_scales = gather("v2_scales", tab2_planes[:], idx2[:], U8)
        for n in range(N // P):
            readings(n)
            take_larger(n)

        v_codes = {}
        for h in range(HALVES):
            v_codes[0, h] = gather("v_codes0%d" % h, tab[0][:].bitcast(U32), part(h), U32)
        w1_q = [quantise("w1q0", group_dealt("w10", w1_raw[0]))]
        v_scales = [gather("v_scales%d" % h, tab_planes[:], part(h), U8) for h in range(HALVES)]
        w1_q.append(quantise("w1q1", group_dealt("w11", w1_raw[1])))
        for h in range(HALVES):
            v_codes[1, h] = gather("v_codes1%d" % h, tab[1][:].bitcast(U32), part(h), U32)

        w3_grouped, w3_q = [], []
        for i in range(units + 5):
            if i < units:
                angle(i)
            if 1 <= i < units + 1:
                cos_of(i - 1)
            if 2 <= i < units + 2:
                marked(i - 2)
            if 3 <= i < units + 3:
                shifted(i - 3)
            if 4 <= i < units + 4:
                group_h(i - 4)
            if i >= 5:
                quantise_h(i - 5)
            if i in (2, 4):
                w3_grouped.append(group_plain("w3%d" % (i // 2 - 1), w3_raw[i // 2 - 1], nc.scalar.copy))
            if i in (4, 6):
                w3_q.append(quantise("w3q%d" % (i // 2 - 2), w3_grouped[i // 2 - 2]))
            if i == 8:
                second_open(0)
                second_close(0)
            if i == 9:
                second_open(1)
        second_close(1)
        for n in range(N // P):
            result = ring.tile([P, PAIRS], F32, name="result")
            nc.vector.tensor_tensor(result[:], y[n][:].indirect(p1[:]), larger[n][:], ALU.mult)
            nc.sync.dma_start(out=out[P * n : P * (n + 1), :], in_=result[:])
